import numpy as np
import ml_dtypes


def mxq(x, axis, fmt="e4m3"):
    dtype, down = {"e4m3": (ml_dtypes.float8_e4m3fn, 7), "e5m2": (ml_dtypes.float8_e5m2, 14)}[fmt]
    v = np.moveaxis(np.asarray(x, np.float32).astype(ml_dtypes.bfloat16).astype(np.float64), axis, -1)
    blocks = v.reshape(v.shape[:-1] + (-1, 32))
    amax = np.abs(blocks).max(-1, keepdims=True)
    byte = np.maximum(np.where(amax > 0, np.frexp(amax)[1] - 1 + 127, 0) - down, 1)
    scale = np.exp2(byte - 127.0)
    codes = (blocks / scale).astype(np.float32).astype(dtype).astype(np.float64)
    return np.moveaxis((codes * scale).reshape(v.shape), -1, axis)


WIDE = False


def mx_kscale(k):
    if not WIDE:
        return np.ones(k)
    levels = np.array([10, -10, 5, -5, 0])
    if k % 512:
        return np.exp2(np.random.permutation(np.resize(levels, k // 32))).repeat(32)
    a = np.empty((k // 512, 16))
    for p in range(k // 512):
        a[p, :8] = np.random.permutation(np.resize(levels, 8))
        for g in range(8):
            far = levels[np.abs(levels - a[p, g]) >= 10]
            a[p, g + 8] = far[np.random.randint(len(far))]
    return np.exp2(a.ravel()).repeat(32)


def f64(x):
    return np.asarray(x).astype(np.float64)


def striped(idx):
    return np.tile(idx.reshape(-1, 16).T, (8, 1)).astype(np.uint16)


def unstriped(offs):
    return offs[:16].T.reshape(-1).astype(np.int64)


def pack_weight(w):
    k, n = w.shape
    w = f64(np.asarray(w, np.float32).astype(ml_dtypes.bfloat16)).reshape(k // 32, 32, n)
    amax = np.abs(w).max(1)
    byte = np.clip(np.where(amax > 0, np.frexp(amax)[1] - 1 + 127 - 7, 1), 1, 254)
    scaled = (w * np.exp2(127.0 - byte)[:, None, :]).reshape(k, n).astype(np.float32)
    words = np.ascontiguousarray(scaled.reshape(k // 512, 128, 4, n).transpose(0, 1, 3, 2)).astype(ml_dtypes.float8_e4m3fn).view(np.uint8)
    return words, np.ascontiguousarray(byte.astype(np.uint8).reshape(k // 512, 16, n))


def unpack_weight(words, scales):
    g, p, n, _ = words.shape
    vals = np.ascontiguousarray(words).view(ml_dtypes.float8_e4m3fn).astype(np.float64) * np.repeat(np.exp2(scales.astype(np.float64) - 127.0), 8, axis=1)[..., None]
    return vals.transpose(0, 1, 3, 2).reshape(g * 512, n)


K, T, S, D, N, W = 512, 2048, 512, 4, 128, 2048
P = 2 ** 7


def setup_inputs():
    n = np.random.standard_normal
    s = mx_kscale(K)[:, None]
    packed_xT = pack_weight(n((K, T)) * s)
    packed_eT = pack_weight(n((K, W)) * s)
    return {
        "x_words": packed_xT[0],
        "x_scales": packed_xT[1],
        "e_words": packed_eT[0],
        "e_scales": packed_eT[1],
        "w1": (n((K, N)) / np.sqrt(K) / s).astype(np.float32),
        "wb": (n((K, N)) / np.sqrt(K) / s).astype(np.float32),
        "mask": (np.tile(np.random.uniform(0.0, 1.0, S), (P, 1))).astype(np.float32),
        "offs": striped(np.random.permutation(T)[:S]),
        "sec": striped(np.random.permutation(W)[:S]),
    }


def reference(x_words, x_scales, e_words, e_scales, w1, wb, mask, offs, sec):
    xq = unpack_weight(x_words, x_scales)[:, unstriped(offs)]
    pa = mxq(f64(w1), 0, "e4m3").T @ xq
    ga = pa.reshape(len(pa), -1, D).mean(axis=2)
    la = pa - np.repeat(ga, D, axis=1)
    e_sec = unpack_weight(e_words, e_scales)[:, unstriped(sec)]
    pb = mxq(f64(wb), 0, "e4m3").T @ e_sec
    gb = pb.reshape(len(pb), -1, D).mean(axis=2)
    lb = pb - np.repeat(gb, D, axis=1)
    gm = f64(mask)[:1].reshape(len(f64(mask)[:1]), -1, D).mean(axis=2)
    low = gm * ga + (-1.0 * gm + 1.0) * gb
    return f64(mask)[:1] * la + (-1.0 * f64(mask)[:1] + 1.0) * lb + np.repeat(low, D, axis=1)

@@ -1,0 +1,167 @@
+from contextlib import ExitStack
+
+import concourse.mybir as mybir
+from concourse.masks import make_identity
+
+F32 = mybir.dt.float32
+BF16 = mybir.dt.bfloat16
+I32 = mybir.dt.int32
+U32 = mybir.dt.uint32
+U16 = mybir.dt.uint16
+U8 = mybir.dt.uint8
+FP8X4 = mybir.dt.float8_e4m3fn_x4
+ALU = mybir.AluOpType
+ACT = mybir.ActivationFunctionType
+AXIS_X = mybir.AxisListType.X
+
+P = 128
+PACK = 4
+K, T, S, D, N = 512, 2048, 512, 4, 128
+V = S // D
+HALVES = 2
+SH = S // HALVES
+VH = V // HALVES
+E_ROW, X_ROW = 0, 4
+
+FLOPS = 2 * 2 * K * N * S
+BYTES = 2 * (K * T + 16 * T) + 2 * 4 * K * N + 4 * S + 2 * 2 * P * (S // 16) + 4 * N * S
+
+
+def tile_picked_yblend_pyr_p_kernel(
+    tc, x_words, x_scales, e_words, e_scales, w1, wb, mask, offs, sec, out
+):
+    nc = tc.nc
+    with ExitStack() as ctx:
+        keep = ctx.enter_context(tc.tile_pool(name="keep", bufs=1))
+        psum = ctx.enter_context(tc.psum_pool(name="psum", bufs=1))
+
+        sec_t = keep.tile([P, S // 16], U16, name="sec_t")
+        offs_t = keep.tile([P, S // 16], U16, name="offs_t")
+        nc.sync.dma_start(sec_t[:], sec)
+        nc.sync.dma_start(offs_t[:], offs)
+
+        mcol = keep.tile([P, D], F32, name="mcol")
+        nc.gpsimd.dma_start(mcol[:], mask[0].rearrange("(v d) -> v d", d=D))
+
+        def scale_window(scales, row, queues, name, tag):
+            win = keep.tile([P, T], U8, name=name, tag=tag, align_bytes=64)
+            nc.vector.memset(win[:].bitcast(I32), 0)
+            for q in range(4):
+                queues[q].dma_start(
+                    win[32 * q + row : 32 * q + row + 4, :].bitcast(I32),
+                    scales[0, 4 * q : 4 * q + 4, :].bitcast(I32),
+                )
+            return win
+
+        def load_words(words, name, tag):
+            win = keep.tile([P, T], I32, name=name, tag=tag, align_bytes=64)
+            nc.sync.dma_start(win[:], words[0].rearrange("p n t -> p (n t)").bitcast(I32))
+            return win
+
+        def load_weight(w, queue, name, tag):
+            raw = keep.tile([P, PACK, N], F32, name=name, tag=tag, align_bytes=64)
+            queue.dma_start(raw[:], w.rearrange("(p j) n -> p j n", j=PACK))
+            return raw
+
+        def quantize(grouped, name):
+            codes = keep.tile([P, N], U32, name=name + "_codes", align_bytes=64)
+            plane = keep.tile([P, N], U8, name=name + "_plane", align_bytes=64)
+            nc.vector.quantize_mx(
+                out=codes[:].bitcast(FP8X4), scales=plane[:], in_=grouped[:].rearrange("p n j -> p (n j)")
+            )
+            return codes, plane
+
+        def gather(window, offsets, dtype, name, tag):
+            picked = keep.tile([P, 16 * offsets.shape[1]], dtype, name=name, tag=tag, align_bytes=64)
+            nc.vector.tensor_copy(picked[:], window.indirect(offsets))
+            return picked
+
+        es_win = scale_window(e_scales, E_ROW, [nc.scalar] * 4, "es_win", "slot_b")
+        xs_win = scale_window(x_scales, X_ROW, [nc.scalar] * 2 + [nc.gpsimd] * 2, "xs_win", "slot_c")
+        wb_raw = load_weight(wb, nc.sync, "wb_raw", "slot_a")
+        ew_win = load_words(e_words, "ew_win", "ew_win")
+
+        ident = keep.tile([P, P], F32, name="ident")
+        make_identity(nc, ident[:])
+
+        wb_grp = keep.tile([P, N, PACK], BF16, name="wb_grp", tag="slot_d", align_bytes=64)
+        nc.vector.tensor_copy(wb_grp[:], wb_raw[:].rearrange("p j n -> p n j"))
+        xw_win = load_words(x_words, "xw_win", "slot_a")
+        wb_codes, wb_plane = quantize(wb_grp, "wb")
+
+        w1_raw = load_weight(w1, nc.scalar, "w1_raw", "slot_d")
+        e_bytes = gather(es_win[:], sec_t[:], U8, "e_bytes", "e_bytes")
+        x_bytes = gather(xs_win[:], offs_t[:], U8, "x_bytes", "slot_b")
+        e_codes = gather(ew_win[:].bitcast(U32), sec_t[:], U32, "e_codes", "slot_c")
+
+        m16 = keep.tile([P, D], F32, name="m16")
+        gm4 = keep.tile([P, 1], F32, name="gm4")
+        ccol = keep.tile([P, D], F32, name="ccol")
+        nc.scalar.activation(m16[:], mcol[:], ACT.Identity, scale=1.0 / 16.0, accum_out=gm4[:])
+        nc.scalar.activation(ccol[:], m16[:], ACT.Identity, bias=gm4[:], scale=-4.0)
+        m_bank = psum.tile([P, D, V], F32, name="m_bank")
+        c_bank = psum.tile([P, D, V], F32, name="c_bank")
+        for d in range(D):
+            nc.tensor.transpose(m_bank[:, d, :], mcol[:, d : d + 1].to_broadcast([P, P]), ident[:])
+        for d in range(D):
+            nc.tensor.transpose(c_bank[:, d, :], ccol[:, d : d + 1].to_broadcast([P, P]), ident[:])
+        om_row = keep.tile([P, V, D], F32, name="om_row")
+        m_row = keep.tile([P, V, D], F32, name="m_row")
+        nc.scalar.activation(om_row[:], m_bank[:].rearrange("p d v -> p v d"), ACT.Copy, bias=1.0, scale=-1.0)
+        nc.scalar.copy(m_row[:], m_bank[:].rearrange("p d v -> p v d"))
+
+        pb = psum.tile([P, V, D], F32, name="pb")
+        nc.tensor.matmul_mx(
+            out=pb[:].rearrange("p v d -> p (v d)"),
+            lhsT=wb_codes[:].bitcast(FP8X4),
+            lhsT_scale=wb_plane[:],
+            rhs=e_codes[:].bitcast(FP8X4),
+            rhs_scale=e_bytes[E_ROW:P, :],
+            start=True,
+            stop=True,
+        )
+        q1 = keep.tile([P, V, D], F32, name="q1")
+        sb = keep.tile([P, V], F32, name="sb")
+        nc.vector.tensor_tensor(q1[:], pb[:], om_row[:], ALU.mult)
+        nc.vector.tensor_reduce(sb[:], pb[:], AXIS_X, ALU.add)
+
+        w1_grp = keep.tile([P, N, PACK], BF16, name="w1_grp", align_bytes=64)
+        nc.scalar.copy(w1_grp[:], w1_raw[:].rearrange("p j n -> p n j"))
+        w1_codes, w1_plane = quantize(w1_grp, "w1")
+
+        pa = []
+        for h in range(HALVES):
+            cols = SH // 16
+            x_codes = gather(xw_win[:].bitcast(U32), offs_t[:, h * cols : (h + 1) * cols], U32, "x_codes%d" % h, "x_codes%d" % h)
+            acc = psum.tile([P, VH, D], F32, name="pa%d" % h)
+            nc.tensor.matmul_mx(
+                out=acc[:].rearrange("p v d -> p (v d)"),
+                lhsT=w1_codes[:].bitcast(FP8X4),
+                lhsT_scale=w1_plane[:],
+                rhs=x_codes[:].bitcast(FP8X4),
+                rhs_scale=x_bytes[X_ROW:P, h * SH : (h + 1) * SH],
+                start=True,
+                stop=True,
+            )
+            pa.append(acc)
+
+        for h in range(HALVES):
+            vs = slice(h * VH, (h + 1) * VH)
+            sa = keep.tile([P, VH], F32, name="sa%d" % h)
+            sd = keep.tile([P, VH], F32, name="sd%d" % h)
+            fine = keep.tile([P, VH, D], F32, name="fine%d" % h)
+            both = keep.tile([P, VH, D], F32, name="both%d" % h)
+            corr = keep.tile([P, VH, D], F32, name="corr%d" % h)
+            res = keep.tile([P, VH, D], F32, name="res%d" % h)
+            nc.vector.tensor_reduce(sa[:], pa[h][:], AXIS_X, ALU.add)
+            nc.vector.tensor_tensor(fine[:], pa[h][:], m_row[:, vs, :], ALU.mult)
+            nc.vector.tensor_tensor(sd[:], sa[:], sb[:, vs], ALU.subtract)
+            nc.vector.tensor_tensor(both[:], fine[:], q1[:, vs, :], ALU.add)
+            nc.vector.tensor_tensor(
+                corr[:],
+                c_bank[:, :, vs].rearrange("p d v -> p v d"),
+                sd[:].unsqueeze(2).to_broadcast([P, VH, D]),
+                ALU.mult,
+            )
+            nc.vector.tensor_tensor(res[:], both[:], corr[:], ALU.add)
+            nc.sync.dma_start(out[:, h * SH : (h + 1) * SH], res[:].rearrange("p v d -> p (v d)"))

@@ -18,13 +18,16 @@ P = 128
 PACK = 4
 K, T, S, D, N = 512, 2048, 512, 4, 128
 V = S // D
+LIST_ROWS = 16
+QUADRANTS, QUADRANT_ROWS = 4, 32
+SCALE_ROWS = 4
 HALVES = 2
 SH = S // HALVES
 VH = V // HALVES
 E_ROW, X_ROW = 0, 4
 
 FLOPS = 2 * 2 * K * N * S
-BYTES = 2 * (K * T + 16 * T) + 2 * 4 * K * N + 4 * S + 2 * 2 * P * (S // 16) + 4 * N * S
+BYTES = 2 * (K * T + (K // 32) * T) + 2 * 4 * K * N + 4 * S + 2 * 2 * P * (S // LIST_ROWS) + 4 * N * S
 
 
 def tile_picked_yblend_pyr_p_kernel(
@@ -33,135 +36,130 @@ def tile_picked_yblend_pyr_p_kernel(
     nc = tc.nc
     with ExitStack() as ctx:
         keep = ctx.enter_context(tc.tile_pool(name="keep", bufs=1))
+        shared = ctx.enter_context(tc.tile_pool(name="shared", bufs=1))
         psum = ctx.enter_context(tc.psum_pool(name="psum", bufs=1))
 
-        sec_t = keep.tile([P, S // 16], U16, name="sec_t")
-        offs_t = keep.tile([P, S // 16], U16, name="offs_t")
-        nc.sync.dma_start(sec_t[:], sec)
-        nc.sync.dma_start(offs_t[:], offs)
-
-        mcol = keep.tile([P, D], F32, name="mcol")
-        nc.gpsimd.dma_start(mcol[:], mask[0].rearrange("(v d) -> v d", d=D))
-
-        def scale_window(scales, row, queues, name, tag):
-            win = keep.tile([P, T], U8, name=name, tag=tag, align_bytes=64)
-            nc.vector.memset(win[:].bitcast(I32), 0)
-            for q in range(4):
-                queues[q].dma_start(
-                    win[32 * q + row : 32 * q + row + 4, :].bitcast(I32),
-                    scales[0, 4 * q : 4 * q + 4, :].bitcast(I32),
+        def load_scales(scales, row, table):
+            nc.vector.memset(table[:].bitcast(I32), 0)
+            for q in range(QUADRANTS):
+                first = QUADRANT_ROWS * q + row
+                nc.sync.dma_start(
+                    table[first : first + SCALE_ROWS, :].bitcast(I32),
+                    scales[0, SCALE_ROWS * q : SCALE_ROWS * (q + 1), :].bitcast(I32),
                 )
-            return win
+            return table
 
-        def load_words(words, name, tag):
-            win = keep.tile([P, T], I32, name=name, tag=tag, align_bytes=64)
-            nc.sync.dma_start(win[:], words[0].rearrange("p n t -> p (n t)").bitcast(I32))
-            return win
+        def load_words(words, name):
+            table = keep.tile([P, T], I32, name=name)
+            nc.sync.dma_start(table[:], words[0].rearrange("p n t -> p (n t)").bitcast(I32))
+            return table
 
-        def load_weight(w, queue, name, tag):
-            raw = keep.tile([P, PACK, N], F32, name=name, tag=tag, align_bytes=64)
-            queue.dma_start(raw[:], w.rearrange("(p j) n -> p j n", j=PACK))
+        def load_weight(w, name):
+            raw = keep.tile([P, PACK, N], F32, name=name)
+            nc.sync.dma_start(raw[:], w.rearrange("(p j) n -> p j n", j=PACK))
             return raw
 
         def quantize(grouped, name):
             codes = keep.tile([P, N], U32, name=name + "_codes", align_bytes=64)
-            plane = keep.tile([P, N], U8, name=name + "_plane", align_bytes=64)
+            scales = keep.tile([P, N], U8, name=name + "_scales", align_bytes=64)
             nc.vector.quantize_mx(
-                out=codes[:].bitcast(FP8X4), scales=plane[:], in_=grouped[:].rearrange("p n j -> p (n j)")
+                out=codes[:].bitcast(FP8X4), scales=scales[:], in_=grouped[:].rearrange("p n j -> p (n j)")
             )
-            return codes, plane
+            return codes, scales
 
-        def gather(window, offsets, dtype, name, tag):
-            picked = keep.tile([P, 16 * offsets.shape[1]], dtype, name=name, tag=tag, align_bytes=64)
-            nc.vector.tensor_copy(picked[:], window.indirect(offsets))
+        def gather(picked, table, offsets):
+            nc.vector.tensor_copy(picked[:], table.indirect(offsets))
             return picked
 
-        es_win = scale_window(e_scales, E_ROW, [nc.scalar] * 4, "es_win", "slot_b")
-        xs_win = scale_window(x_scales, X_ROW, [nc.scalar] * 2 + [nc.gpsimd] * 2, "xs_win", "slot_c")
-        wb_raw = load_weight(wb, nc.sync, "wb_raw", "slot_a")
-        ew_win = load_words(e_words, "ew_win", "ew_win")
-
-        ident = keep.tile([P, P], F32, name="ident")
-        make_identity(nc, ident[:])
-
-        wb_grp = keep.tile([P, N, PACK], BF16, name="wb_grp", tag="slot_d", align_bytes=64)
-        nc.vector.tensor_copy(wb_grp[:], wb_raw[:].rearrange("p j n -> p n j"))
-        xw_win = load_words(x_words, "xw_win", "slot_a")
-        wb_codes, wb_plane = quantize(wb_grp, "wb")
-
-        w1_raw = load_weight(w1, nc.scalar, "w1_raw", "slot_d")
-        e_bytes = gather(es_win[:], sec_t[:], U8, "e_bytes", "e_bytes")
-        x_bytes = gather(xs_win[:], offs_t[:], U8, "x_bytes", "slot_b")
-        e_codes = gather(ew_win[:].bitcast(U32), sec_t[:], U32, "e_codes", "slot_c")
-
-        m16 = keep.tile([P, D], F32, name="m16")
-        gm4 = keep.tile([P, 1], F32, name="gm4")
-        ccol = keep.tile([P, D], F32, name="ccol")
-        nc.scalar.activation(m16[:], mcol[:], ACT.Identity, scale=1.0 / 16.0, accum_out=gm4[:])
-        nc.scalar.activation(ccol[:], m16[:], ACT.Identity, bias=gm4[:], scale=-4.0)
-        m_bank = psum.tile([P, D, V], F32, name="m_bank")
-        c_bank = psum.tile([P, D, V], F32, name="c_bank")
-        for d in range(D):
-            nc.tensor.transpose(m_bank[:, d, :], mcol[:, d : d + 1].to_broadcast([P, P]), ident[:])
-        for d in range(D):
-            nc.tensor.transpose(c_bank[:, d, :], ccol[:, d : d + 1].to_broadcast([P, P]), ident[:])
-        om_row = keep.tile([P, V, D], F32, name="om_row")
-        m_row = keep.tile([P, V, D], F32, name="m_row")
-        nc.scalar.activation(om_row[:], m_bank[:].rearrange("p d v -> p v d"), ACT.Copy, bias=1.0, scale=-1.0)
-        nc.scalar.copy(m_row[:], m_bank[:].rearrange("p d v -> p v d"))
-
-        pb = psum.tile([P, V, D], F32, name="pb")
-        nc.tensor.matmul_mx(
-            out=pb[:].rearrange("p v d -> p (v d)"),
-            lhsT=wb_codes[:].bitcast(FP8X4),
-            lhsT_scale=wb_plane[:],
-            rhs=e_codes[:].bitcast(FP8X4),
-            rhs_scale=e_bytes[E_ROW:P, :],
-            start=True,
-            stop=True,
-        )
-        q1 = keep.tile([P, V, D], F32, name="q1")
-        sb = keep.tile([P, V], F32, name="sb")
-        nc.vector.tensor_tensor(q1[:], pb[:], om_row[:], ALU.mult)
-        nc.vector.tensor_reduce(sb[:], pb[:], AXIS_X, ALU.add)
-
-        w1_grp = keep.tile([P, N, PACK], BF16, name="w1_grp", align_bytes=64)
-        nc.scalar.copy(w1_grp[:], w1_raw[:].rearrange("p j n -> p n j"))
-        w1_codes, w1_plane = quantize(w1_grp, "w1")
-
-        pa = []
-        for h in range(HALVES):
-            cols = SH // 16
-            x_codes = gather(xw_win[:].bitcast(U32), offs_t[:, h * cols : (h + 1) * cols], U32, "x_codes%d" % h, "x_codes%d" % h)
-            acc = psum.tile([P, VH, D], F32, name="pa%d" % h)
+        def product(acc, weight, codes, scale_bytes, start, stop):
             nc.tensor.matmul_mx(
                 out=acc[:].rearrange("p v d -> p (v d)"),
-                lhsT=w1_codes[:].bitcast(FP8X4),
-                lhsT_scale=w1_plane[:],
-                rhs=x_codes[:].bitcast(FP8X4),
-                rhs_scale=x_bytes[X_ROW:P, h * SH : (h + 1) * SH],
-                start=True,
-                stop=True,
+                lhsT=weight[0][:].bitcast(FP8X4),
+                lhsT_scale=weight[1][:],
+                rhs=codes.bitcast(FP8X4),
+                rhs_scale=scale_bytes,
+                start=start,
+                stop=stop,
             )
-            pa.append(acc)
 
+        sec_t = keep.tile([P, S // LIST_ROWS], U16, name="sec_t")
+        offs_t = keep.tile([P, S // LIST_ROWS], U16, name="offs_t")
+        nc.sync.dma_start(sec_t[:], sec)
+        wb_raw = load_weight(wb, "wb_raw")
+        w1_raw = load_weight(w1, "w1_raw")
+        e_scale_table = load_scales(e_scales, E_ROW, keep.tile([P, T], U8, name="e_scale_table"))
+        ident = keep.tile([P, P], F32, name="ident")
+        make_identity(nc, ident[:])
+        e_word_table = load_words(e_words, "e_word_table")
+        mask_groups = keep.tile([P, D], F32, name="mask_groups")
+        nc.sync.dma_start(mask_groups[:], mask[0].rearrange("(v d) -> v d", d=D))
+        nc.sync.dma_start(offs_t[:], offs)
+        x_scale_table = load_scales(x_scales, X_ROW, shared.tile([P, T], U8, name="x_scale_table", offset=0))
+
+        wb_grouped = keep.tile([P, N, PACK], BF16, name="wb_grouped", align_bytes=64)
+        nc.vector.tensor_copy(wb_grouped[:], wb_raw[:].rearrange("p j n -> p n j"))
+        wb_mx = quantize(wb_grouped, "wb")
+        w1_grouped = keep.tile([P, N, PACK], BF16, name="w1_grouped", align_bytes=64)
+        nc.scalar.activation(w1_grouped[:], w1_raw[:].rearrange("p j n -> p n j"), ACT.Copy, scale=-1.0)
+
+        x_word_table = load_words(x_words, "x_word_table")
+        mask_rows = keep.tile([P, V, D], F32, name="mask_rows")
+        nc.sync.dma_start(mask_rows[:].rearrange("p v d -> p (v d)"), mask)
+
+        e_bytes = gather(keep.tile([P, S], U8, name="e_bytes", align_bytes=64), e_scale_table[:], sec_t[:])
+        w1_mx = quantize(w1_grouped, "w1")
+        e_codes = gather(keep.tile([P, S], U32, name="e_codes", align_bytes=64), e_word_table[:].bitcast(U32), sec_t[:])
+        x_bytes = gather(keep.tile([P, S], U8, name="x_bytes", align_bytes=64), x_scale_table[:], offs_t[:])
+
+        neg_mask16 = keep.tile([P, D], F32, name="neg_mask16")
+        neg_gm4 = keep.tile([P, 1], F32, name="neg_gm4")
+        neg_c_groups = keep.tile([P, D], F32, name="neg_c_groups")
+        nc.scalar.activation(neg_mask16[:], mask_groups[:], ACT.Identity, scale=-1.0 / (D * D), accum_out=neg_gm4[:])
+        nc.scalar.activation(neg_c_groups[:], neg_mask16[:], ACT.Identity, bias=neg_gm4[:], scale=-float(D))
+        neg_c = psum.tile([P, D, V], F32, name="neg_c")
+        for d in range(D):
+            nc.tensor.transpose(neg_c[:, d, :], neg_c_groups[:, d : d + 1].to_broadcast([P, P]), ident[:])
+
+        pb = psum.tile([P, V, D], F32, name="pb")
+        product(pb, wb_mx, e_codes[:], e_bytes[E_ROW:P, :], True, True)
+        neg_pa0 = psum.tile([P, VH, D], F32, name="neg_pa0")
+        nd1 = psum.tile([P, VH, D], F32, name="nd1")
+        product(nd1, wb_mx, e_codes[:, SH:S], e_bytes[E_ROW:P, SH:S], True, False)
+        pb_sb = keep.tile([P, V, D], F32, name="pb_sb")
+        nc.scalar.copy(pb_sb[:], pb[:])
+
+        list_cols = SH // LIST_ROWS
+        for h, acc in enumerate((neg_pa0, nd1)):
+            picked = shared.tile([P, SH], U32, name="x_codes%d" % h, offset=h * SH * PACK, align_bytes=64)
+            x_codes = gather(picked, x_word_table[:].bitcast(U32), offs_t[:, h * list_cols : (h + 1) * list_cols])
+            product(acc, w1_mx, x_codes[:], x_bytes[X_ROW:P, h * SH : (h + 1) * SH], acc is neg_pa0, True)
+
+        def half_tiles(name):
+            return [keep.tile([P, VH, D], F32, name="%s%d" % (name, h)) for h in range(HALVES)]
+
+        groups = [slice(h * VH, (h + 1) * VH) for h in range(HALVES)]
+        nd0 = keep.tile([P, VH, D], F32, name="nd0")
+        masked = half_tiles("masked")
+        coarse = half_tiles("coarse")
+        partial = half_tiles("partial")
+        result = half_tiles("result")
+        neg_s = [keep.tile([P, VH], F32, name="neg_s%d" % h) for h in range(HALVES)]
+
+        nc.vector.tensor_tensor(nd0[:], neg_pa0[:], pb_sb[:, groups[0], :], ALU.add)
+        nc.gpsimd.tensor_tensor(masked[0][:], nd0[:], mask_rows[:, groups[0], :], ALU.mult)
+        nc.vector.tensor_tensor(masked[1][:], nd1[:], mask_rows[:, groups[1], :], ALU.mult)
+        nc.gpsimd.tensor_tensor(partial[1][:], pb_sb[:, groups[1], :], masked[1][:], ALU.subtract)
+        for h, nd in enumerate((nd0, nd1)):
+            nc.vector.tensor_reduce(neg_s[h][:], nd[:], AXIS_X, ALU.add)
         for h in range(HALVES):
-            vs = slice(h * VH, (h + 1) * VH)
-            sa = keep.tile([P, VH], F32, name="sa%d" % h)
-            sd = keep.tile([P, VH], F32, name="sd%d" % h)
-            fine = keep.tile([P, VH, D], F32, name="fine%d" % h)
-            both = keep.tile([P, VH, D], F32, name="both%d" % h)
-            corr = keep.tile([P, VH, D], F32, name="corr%d" % h)
-            res = keep.tile([P, VH, D], F32, name="res%d" % h)
-            nc.vector.tensor_reduce(sa[:], pa[h][:], AXIS_X, ALU.add)
-            nc.vector.tensor_tensor(fine[:], pa[h][:], m_row[:, vs, :], ALU.mult)
-            nc.vector.tensor_tensor(sd[:], sa[:], sb[:, vs], ALU.subtract)
-            nc.vector.tensor_tensor(both[:], fine[:], q1[:, vs, :], ALU.add)
             nc.vector.tensor_tensor(
-                corr[:],
-                c_bank[:, :, vs].rearrange("p d v -> p v d"),
-                sd[:].unsqueeze(2).to_broadcast([P, VH, D]),
+                coarse[h][:],
+                neg_c[:, :, groups[h]].rearrange("p d v -> p v d"),
+                neg_s[h][:].unsqueeze(2).to_broadcast([P, VH, D]),
                 ALU.mult,
             )
-            nc.vector.tensor_tensor(res[:], both[:], corr[:], ALU.add)
-            nc.sync.dma_start(out[:, h * SH : (h + 1) * SH], res[:].rearrange("p v d -> p (v d)"))
+        nc.vector.tensor_tensor(partial[0][:], pb[:, groups[0], :], coarse[0][:], ALU.add)
+        nc.vector.tensor_tensor(result[1][:], partial[1][:], coarse[1][:], ALU.add)
+        nc.vector.tensor_tensor(result[0][:], partial[0][:], masked[0][:], ALU.subtract)
+        for h in reversed(range(HALVES)):
+            nc.sync.dma_start(out[:, h * SH : (h + 1) * SH], result[h][:].rearrange("p v d -> p (v d)"))

from contextlib import ExitStack

import concourse.mybir as mybir
from concourse.masks import make_identity

F32 = mybir.dt.float32
BF16 = mybir.dt.bfloat16
I32 = mybir.dt.int32
U32 = mybir.dt.uint32
U16 = mybir.dt.uint16
U8 = mybir.dt.uint8
FP8X4 = mybir.dt.float8_e4m3fn_x4
ALU = mybir.AluOpType
ACT = mybir.ActivationFunctionType
AXIS_X = mybir.AxisListType.X

P = 128
PACK = 4
K, T, S, D, N = 512, 2048, 512, 4, 128
V = S // D
LIST_ROWS = 16
QUADRANTS, QUADRANT_ROWS = 4, 32
SCALE_ROWS = 4
HALVES = 2
SH = S // HALVES
VH = V // HALVES
E_ROW, X_ROW = 0, 4

FLOPS = 2 * 2 * K * N * S
BYTES = 2 * (K * T + (K // 32) * T) + 2 * 4 * K * N + 4 * S + 2 * 2 * P * (S // LIST_ROWS) + 4 * N * S


def tile_picked_yblend_pyr_p_kernel(
    tc, x_words, x_scales, e_words, e_scales, w1, wb, mask, offs, sec, out
):
    nc = tc.nc
    with ExitStack() as ctx:
        keep = ctx.enter_context(tc.tile_pool(name="keep", bufs=1))
        shared = ctx.enter_context(tc.tile_pool(name="shared", bufs=1))
        psum = ctx.enter_context(tc.psum_pool(name="psum", bufs=1))

        def load_scales(scales, row, table):
            nc.vector.memset(table[:].bitcast(I32), 0)
            for q in range(QUADRANTS):
                first = QUADRANT_ROWS * q + row
                nc.sync.dma_start(
                    table[first : first + SCALE_ROWS, :].bitcast(I32),
                    scales[0, SCALE_ROWS * q : SCALE_ROWS * (q + 1), :].bitcast(I32),
                )
            return table

        def load_words(words, name):
            table = keep.tile([P, T], I32, name=name)
            nc.sync.dma_start(table[:], words[0].rearrange("p n t -> p (n t)").bitcast(I32))
            return table

        def load_weight(w, name):
            raw = keep.tile([P, PACK, N], F32, name=name)
            nc.sync.dma_start(raw[:], w.rearrange("(p j) n -> p j n", j=PACK))
            return raw

        def quantize(grouped, name):
            codes = keep.tile([P, N], U32, name=name + "_codes", align_bytes=64)
            scales = keep.tile([P, N], U8, name=name + "_scales", align_bytes=64)
            nc.vector.quantize_mx(
                out=codes[:].bitcast(FP8X4), scales=scales[:], in_=grouped[:].rearrange("p n j -> p (n j)")
            )
            return codes, scales

        def gather(picked, table, offsets):
            nc.vector.tensor_copy(picked[:], table.indirect(offsets))
            return picked

        def product(acc, weight, codes, scale_bytes, start, stop):
            nc.tensor.matmul_mx(
                out=acc[:].rearrange("p v d -> p (v d)"),
                lhsT=weight[0][:].bitcast(FP8X4),
                lhsT_scale=weight[1][:],
                rhs=codes.bitcast(FP8X4),
                rhs_scale=scale_bytes,
                start=start,
                stop=stop,
            )

        sec_t = keep.tile([P, S // LIST_ROWS], U16, name="sec_t")
        offs_t = keep.tile([P, S // LIST_ROWS], U16, name="offs_t")
        nc.sync.dma_start(sec_t[:], sec)
        wb_raw = load_weight(wb, "wb_raw")
        w1_raw = load_weight(w1, "w1_raw")
        e_scale_table = load_scales(e_scales, E_ROW, keep.tile([P, T], U8, name="e_scale_table"))
        ident = keep.tile([P, P], F32, name="ident")
        make_identity(nc, ident[:])
        e_word_table = load_words(e_words, "e_word_table")
        mask_groups = keep.tile([P, D], F32, name="mask_groups")
        nc.sync.dma_start(mask_groups[:], mask[0].rearrange("(v d) -> v d", d=D))
        nc.sync.dma_start(offs_t[:], offs)
        x_scale_table = load_scales(x_scales, X_ROW, shared.tile([P, T], U8, name="x_scale_table", offset=0))

        wb_grouped = keep.tile([P, N, PACK], BF16, name="wb_grouped", align_bytes=64)
        nc.vector.tensor_copy(wb_grouped[:], wb_raw[:].rearrange("p j n -> p n j"))
        wb_mx = quantize(wb_grouped, "wb")
        w1_grouped = keep.tile([P, N, PACK], BF16, name="w1_grouped", align_bytes=64)
        nc.scalar.activation(w1_grouped[:], w1_raw[:].rearrange("p j n -> p n j"), ACT.Copy, scale=-1.0)

        x_word_table = load_words(x_words, "x_word_table")
        mask_rows = keep.tile([P, V, D], F32, name="mask_rows")
        nc.sync.dma_start(mask_rows[:].rearrange("p v d -> p (v d)"), mask)

        e_bytes = gather(keep.tile([P, S], U8, name="e_bytes", align_bytes=64), e_scale_table[:], sec_t[:])
        w1_mx = quantize(w1_grouped, "w1")
        e_codes = gather(keep.tile([P, S], U32, name="e_codes", align_bytes=64), e_word_table[:].bitcast(U32), sec_t[:])
        x_bytes = gather(keep.tile([P, S], U8, name="x_bytes", align_bytes=64), x_scale_table[:], offs_t[:])

        neg_mask16 = keep.tile([P, D], F32, name="neg_mask16")
        neg_gm4 = keep.tile([P, 1], F32, name="neg_gm4")
        neg_c_groups = keep.tile([P, D], F32, name="neg_c_groups")
        nc.scalar.activation(neg_mask16[:], mask_groups[:], ACT.Identity, scale=-1.0 / (D * D), accum_out=neg_gm4[:])
        nc.scalar.activation(neg_c_groups[:], neg_mask16[:], ACT.Identity, bias=neg_gm4[:], scale=-float(D))
        neg_c = psum.tile([P, D, V], F32, name="neg_c")
        for d in range(D):
            nc.tensor.transpose(neg_c[:, d, :], neg_c_groups[:, d : d + 1].to_broadcast([P, P]), ident[:])

        pb = psum.tile([P, V, D], F32, name="pb")
        product(pb, wb_mx, e_codes[:], e_bytes[E_ROW:P, :], True, True)
        neg_pa0 = psum.tile([P, VH, D], F32, name="neg_pa0")
        nd1 = psum.tile([P, VH, D], F32, name="nd1")
        product(nd1, wb_mx, e_codes[:, SH:S], e_bytes[E_ROW:P, SH:S], True, False)
        pb_sb = keep.tile([P, V, D], F32, name="pb_sb")
        nc.scalar.copy(pb_sb[:], pb[:])

        list_cols = SH // LIST_ROWS
        for h, acc in enumerate((neg_pa0, nd1)):
            picked = shared.tile([P, SH], U32, name="x_codes%d" % h, offset=h * SH * PACK, align_bytes=64)
            x_codes = gather(picked, x_word_table[:].bitcast(U32), offs_t[:, h * list_cols : (h + 1) * list_cols])
            product(acc, w1_mx, x_codes[:], x_bytes[X_ROW:P, h * SH : (h + 1) * SH], acc is neg_pa0, True)

        def half_tiles(name):
            return [keep.tile([P, VH, D], F32, name="%s%d" % (name, h)) for h in range(HALVES)]

        groups = [slice(h * VH, (h + 1) * VH) for h in range(HALVES)]
        nd0 = keep.tile([P, VH, D], F32, name="nd0")
        masked = half_tiles("masked")
        coarse = half_tiles("coarse")
        partial = half_tiles("partial")
        result = half_tiles("result")
        neg_s = [keep.tile([P, VH], F32, name="neg_s%d" % h) for h in range(HALVES)]

        nc.vector.tensor_tensor(nd0[:], neg_pa0[:], pb_sb[:, groups[0], :], ALU.add)
        nc.gpsimd.tensor_tensor(masked[0][:], nd0[:], mask_rows[:, groups[0], :], ALU.mult)
        nc.vector.tensor_tensor(masked[1][:], nd1[:], mask_rows[:, groups[1], :], ALU.mult)
        nc.gpsimd.tensor_tensor(partial[1][:], pb_sb[:, groups[1], :], masked[1][:], ALU.subtract)
        for h, nd in enumerate((nd0, nd1)):
            nc.vector.tensor_reduce(neg_s[h][:], nd[:], AXIS_X, ALU.add)
        for h in range(HALVES):
            nc.vector.tensor_tensor(
                coarse[h][:],
                neg_c[:, :, groups[h]].rearrange("p d v -> p v d"),
                neg_s[h][:].unsqueeze(2).to_broadcast([P, VH, D]),
                ALU.mult,
            )
        nc.vector.tensor_tensor(partial[0][:], pb[:, groups[0], :], coarse[0][:], ALU.add)
        nc.vector.tensor_tensor(result[1][:], partial[1][:], coarse[1][:], ALU.add)
        nc.vector.tensor_tensor(result[0][:], partial[0][:], masked[0][:], ALU.subtract)
        for h in reversed(range(HALVES)):
            nc.sync.dma_start(out[:, h * SH : (h + 1) * SH], result[h][:].rearrange("p v d -> p (v d)"))
